import numpy as np
import ml_dtypes


def mxq(x, axis, fmt="e4m3"):
    dtype, down = {"e4m3": (ml_dtypes.float8_e4m3fn, 7), "e5m2": (ml_dtypes.float8_e5m2, 14)}[fmt]
    v = np.moveaxis(np.asarray(x, np.float32).astype(ml_dtypes.bfloat16).astype(np.float64), axis, -1)
    blocks = v.reshape(v.shape[:-1] + (-1, 32))
    amax = np.abs(blocks).max(-1, keepdims=True)
    byte = np.maximum(np.where(amax > 0, np.frexp(amax)[1] - 1 + 127, 0) - down, 1)
    scale = np.exp2(byte - 127.0)
    codes = (blocks / scale).astype(np.float32).astype(dtype).astype(np.float64)
    return np.moveaxis((codes * scale).reshape(v.shape), -1, axis)


WIDE = False


def mx_kscale(k):
    if not WIDE:
        return np.ones(k)
    levels = np.array([10, -10, 5, -5, 0])
    if k % 512:
        return np.exp2(np.random.permutation(np.resize(levels, k // 32))).repeat(32)
    a = np.empty((k // 512, 16))
    for p in range(k // 512):
        a[p, :8] = np.random.permutation(np.resize(levels, 8))
        for g in range(8):
            far = levels[np.abs(levels - a[p, g]) >= 10]
            a[p, g + 8] = far[np.random.randint(len(far))]
    return np.exp2(a.ravel()).repeat(32)


def f64(x):
    return np.asarray(x).astype(np.float64)


def striped(idx):
    return np.tile(np.asarray(idx).reshape(-1, 16).T, (8, 1)).astype(np.uint16)


def unstriped(offs):
    return offs[:16].T.reshape(-1).astype(np.int64)


E2M1 = np.array([0.0, 0.5, 1.0, 1.5, 2.0, 3.0, 4.0, 6.0, -0.0, -0.5, -1.0, -1.5, -2.0, -3.0, -4.0, -6.0])


def pack_weight(w, fmt):
    k, n = w.shape
    w = f64(np.asarray(w, np.float32).astype(ml_dtypes.bfloat16)).reshape(k // 32, 32, n)
    amax = np.abs(w).max(1)
    if fmt == "e4m3":
        byte = np.frexp(amax)[1] - 1 + 127 - 7
    else:
        mant, ex = np.frexp(amax / 6.0)
        byte = np.where(mant > 0.5, ex, ex - 1) + 127
    byte = np.clip(np.where(amax > 0, byte, 1), 1, 254)
    scaled = (w * np.exp2(127.0 - byte)[:, None, :]).reshape(k, n).astype(np.float32)
    by_word = np.ascontiguousarray(scaled.reshape(k // 512, 128, 4, n).transpose(0, 1, 3, 2))
    if fmt == "e4m3":
        words = by_word.astype(ml_dtypes.float8_e4m3fn).view(np.uint8)
    else:
        c = by_word.astype(ml_dtypes.float4_e2m1fn).view(np.uint8) & 0xF
        words = (c[..., 0::2] | (c[..., 1::2] << 4)).reshape(k // 512, 128, 2 * n)
    return np.ascontiguousarray(words), np.ascontiguousarray(byte.astype(np.uint8).reshape(k // 512, 16, n))


def unpack_weight(words, scales, fmt):
    g, _, n = scales.shape
    words = np.ascontiguousarray(words).reshape(g, 128, n, -1)
    if fmt == "e4m3":
        vals = words.view(ml_dtypes.float8_e4m3fn).astype(np.float64)
    else:
        nib = np.empty((g, 128, n, 4), np.uint8)
        nib[..., 0::2] = words & 0xF
        nib[..., 1::2] = words >> 4
        vals = E2M1[nib]
    vals = vals * np.repeat(np.exp2(scales.astype(np.float64) - 127.0), 8, axis=1)[..., None]
    return vals.transpose(0, 1, 3, 2).reshape(g * 512, n)


B, N, T, D, DV, NQ = 1, 512, 2048, 512, 256, 128


def setup_inputs():
    n = np.random.standard_normal
    idx = np.sort(np.random.permutation(T)[:B * N].reshape(B, N), axis=1).reshape(-1)
    s = mx_kscale(D)[:, None]
    u = np.ones(T)
    u[idx] = mx_kscale(B * N)
    r = np.random.uniform(0.5, 2.0, T)
    qp = [pack_weight(x, "e4m3") for x in n((B, D, NQ)) * s * (0.80 / np.sqrt(D))]
    k = n((D, T)) / s
    v = n((DV, T)) / (u * r)
    kp = pack_weight(k, "e4m3")
    return {
        "q_words": np.stack([x[0] for x in qp]),
        "q_scales": np.stack([x[1] for x in qp]),
        "k_words": kp[0],
        "k_scales": kp[1],
        "vT": v.astype(np.float32),
        "vs": np.tile(u * r, (128, 1)).astype(np.float32),
        "og": n((B, NQ, DV)).astype(np.float32),
        "offs": striped(idx),
    }


def reference(q_words, q_scales, k_words, k_scales, vT, vs, og, offs):
    idx = unstriped(offs)
    k = unpack_weight(k_words, k_scales, "e4m3")
    v = f64(vT)
    pick = lambda x: x[:, idx].reshape(x.shape[0], B, N).transpose(1, 0, 2)
    q = np.stack([unpack_weight(q_words[b], q_scales[b], "e4m3") for b in range(B)])
    score = q.transpose(0, 2, 1) @ pick(k)
    p = score / (1.0 + np.exp(-score))
    w = p * pick(f64(vs))[:, :1, :]
    y = mxq(w, 2, "e4m3") @ mxq(pick(v).transpose(0, 2, 1), 1, "e4m3")
    y = y / 16.0
    y = y / (1.0 + np.exp(-f64(og)))
    return y

@@ -1,0 +1,106 @@
+from contextlib import ExitStack
+
+import concourse.mybir as mybir
+from concourse.masks import make_identity
+
+F32 = mybir.dt.float32
+BF16 = mybir.dt.bfloat16
+I32 = mybir.dt.int32
+U32 = mybir.dt.uint32
+U16 = mybir.dt.uint16
+U8 = mybir.dt.uint8
+FP8X4 = mybir.dt.float8_e4m3fn_x4
+ACT = mybir.ActivationFunctionType
+MULT = mybir.AluOpType.mult
+
+P = 128
+PACK = 4
+SLOTS, TOKENS, D, DV, NQ = 512, 2048, 512, 256, 128
+VS_ROW = 8
+
+FLOPS = 2 * NQ * SLOTS * D + 2 * NQ * SLOTS * DV
+BYTES = D * TOKENS + D // 32 * TOKENS + D * NQ + D // 32 * NQ + 4 * DV * TOKENS + 4 * TOKENS + 2 * 4 * NQ * DV + 2 * P * SLOTS // 16
+
+
+def tile_attend_silu_gate_srtq128n512t2048_kernel(tc, q_words, q_scales, k_words, k_scales, vT, vs, og, offs, out):
+    nc = tc.nc
+    halves = DV // P
+    with ExitStack() as ctx:
+        sb = ctx.enter_context(tc.tile_pool(name="sb", bufs=1))
+        ps = ctx.enter_context(tc.psum_pool(name="ps", bufs=1))
+
+        offsets = sb.tile([P, SLOTS // 16], U16, name="offsets")
+        k_pool = sb.tile([P, TOKENS], U32, name="k_pool", align_bytes=64)
+        ks_pool = sb.tile([P, TOKENS], U8, name="ks_pool", align_bytes=64)
+        vs_pool = sb.tile([P, TOKENS], F32, name="vs_pool", align_bytes=64)
+        v_pool = [sb.tile([P, TOKENS], F32, name="v_pool%d" % h, align_bytes=64) for h in range(halves)]
+        q_codes = sb.tile([P, NQ], U32, name="q_codes", align_bytes=64)
+        q_plane = sb.tile([P, NQ], U8, name="q_plane", align_bytes=64)
+        og_sb = sb.tile([P, DV], F32, name="og_sb", align_bytes=64)
+        ident = sb.tile([P, P], F32, name="ident", align_bytes=64)
+
+        nc.vector.memset(ks_pool[:].bitcast(I32), 0)
+        nc.vector.memset(vs_pool[:], 0.0)
+        nc.gpsimd.memset(q_plane[:].bitcast(I32), 0)
+        make_identity(nc, ident[:])
+
+        nc.sync.dma_start(offsets[:], offs)
+        nc.sync.dma_start(q_codes[:].bitcast(I32), q_words[0, 0].rearrange("g q r -> g (q r)").bitcast(I32))
+        for quad in range(4):
+            nc.scalar.dma_start(ks_pool[:].bitcast(I32)[32 * quad : 32 * quad + 4, :], k_scales[0, 4 * quad : 4 * quad + 4, :].bitcast(I32))
+        nc.sync.dma_start(k_pool[:].bitcast(I32), k_words[0].rearrange("g t r -> g (t r)").bitcast(I32))
+        nc.sync.dma_start(v_pool[0][:], vT[0:P, :])
+        nc.scalar.dma_start(vs_pool[VS_ROW : VS_ROW + 1, :], vs[0:1, :])
+        nc.sync.dma_start(v_pool[1][:], vT[P : 2 * P, :])
+        for quad in range(4):
+            nc.scalar.dma_start(q_plane[:].bitcast(I32)[32 * quad : 32 * quad + 4, :], q_scales[0, 0, 4 * quad : 4 * quad + 4, :].bitcast(I32))
+        nc.sync.dma_start(og_sb[:], og[0])
+
+        ks_g = sb.tile([P, SLOTS], U8, name="ks_g", align_bytes=64)
+        nc.vector.tensor_copy(ks_g[:], ks_pool[:].indirect(offsets[:]))
+        k_plane = sb.tile([P, PACK, P], U8, name="k_plane", align_bytes=64)
+        nc.vector.tensor_copy(k_plane[:].rearrange("p t s -> p s t"), ks_g[:].rearrange("p (s t) -> p s t", t=PACK))
+        vs_g = sb.tile([P, SLOTS], F32, name="vs_g", align_bytes=64)
+        nc.vector.tensor_copy(vs_g[:], vs_pool[:].indirect(offsets[:]))
+        k_codes = sb.tile([P, PACK, P], U32, name="k_codes", align_bytes=64)
+        nc.vector.tensor_copy(k_codes[:].rearrange("p t s -> p s t"), k_pool[:].indirect(offsets[:]))
+
+        vs_bank = ps.tile([P, PACK, P], F32, name="vs_bank")
+        for t in range(PACK):
+            nc.tensor.transpose(vs_bank[:, t, :], vs_g[:, t:SLOTS:PACK], ident[:])
+
+        scores = ps.tile([P, PACK, NQ], F32, name="scores")
+        for t in range(PACK):
+            nc.tensor.matmul_mx(out=scores[:, t, :], lhsT=k_codes[:, t, :].bitcast(FP8X4), lhsT_scale=k_plane[:, t, :],
+                                rhs=q_codes[:].bitcast(FP8X4), rhs_scale=q_plane[:], start=True, stop=True)
+        p_sb = sb.tile([P, NQ, PACK], F32, name="p_sb", align_bytes=64)
+        nc.scalar.activation(p_sb[:], scores[:].rearrange("p t q -> p q t"), ACT.Silu)
+        w_bf = sb.tile([P, NQ, PACK], BF16, name="w_bf", align_bytes=64)
+        vs_cols = vs_bank[:, :, VS_ROW : VS_ROW + 1].rearrange("p t o -> p o t").to_broadcast([P, NQ, PACK])
+        nc.vector.tensor_tensor(w_bf[:], p_sb[:], vs_cols, MULT)
+        w_codes = sb.tile([P, NQ], U32, name="w_codes", align_bytes=64)
+        w_plane = sb.tile([P, NQ], U8, name="w_plane", align_bytes=64)
+        nc.vector.quantize_mx(out=w_codes[:].bitcast(FP8X4), scales=w_plane[:], in_=w_bf[:].rearrange("p q t -> p (q t)"))
+
+        gate = sb.tile([P, DV], F32, name="gate", align_bytes=64)
+        nc.scalar.activation(gate[:], og_sb[:], ACT.Sigmoid)
+
+        for h in range(halves):
+            cols = slice(h * P, (h + 1) * P)
+            v_g = sb.tile([P, SLOTS], BF16, name="v_g%d" % h, align_bytes=64)
+            nc.vector.tensor_copy(v_g[:], v_pool[h][:].indirect(offsets[:]))
+            pairs = v_g[:].bitcast(F32)
+            v_bank = ps.tile([P, 2, P], F32, name="v_bank%d" % h)
+            for u in range(2):
+                nc.tensor.transpose(v_bank[:, u, :], pairs[:, u : SLOTS // 2 : 2], ident[:])
+            v_bf = sb.tile([P, P * PACK], BF16, name="v_bf%d" % h, align_bytes=64)
+            nc.scalar.copy(v_bf[:].bitcast(F32).rearrange("p (e u) -> p e u", u=2), v_bank[:].rearrange("p u e -> p e u"))
+            v_codes = sb.tile([P, P], U32, name="v_codes%d" % h, align_bytes=64)
+            v_plane = sb.tile([P, P], U8, name="v_plane%d" % h, align_bytes=64)
+            nc.vector.quantize_mx(out=v_codes[:].bitcast(FP8X4), scales=v_plane[:], in_=v_bf[:])
+            y_bank = ps.tile([P, P], F32, name="y_bank%d" % h)
+            nc.tensor.matmul_mx(out=y_bank[:], lhsT=w_codes[:].bitcast(FP8X4), lhsT_scale=w_plane[:],
+                                rhs=v_codes[:].bitcast(FP8X4), rhs_scale=v_plane[:], start=True, stop=True)
+            res = sb.tile([P, P], F32, name="res%d" % h, align_bytes=64)
+            nc.vector.scalar_tensor_tensor(res[:], y_bank[:], 1.0 / 16.0, gate[:, cols], MULT, MULT)
+            nc.sync.dma_start(out[0, :, cols], res[:])

@@ -27,80 +27,90 @@ def tile_attend_silu_gate_srtq128n512t2048_kernel(tc, q_words, q_scales, k_words
     halves = DV // P
     with ExitStack() as ctx:
         sb = ctx.enter_context(tc.tile_pool(name="sb", bufs=1))
+        reuse = ctx.enter_context(tc.tile_pool(name="reuse", bufs=1))
         ps = ctx.enter_context(tc.psum_pool(name="ps", bufs=1))
 
         offsets = sb.tile([P, SLOTS // 16], U16, name="offsets")
         k_pool = sb.tile([P, TOKENS], U32, name="k_pool", align_bytes=64)
         ks_pool = sb.tile([P, TOKENS], U8, name="ks_pool", align_bytes=64)
         vs_pool = sb.tile([P, TOKENS], F32, name="vs_pool", align_bytes=64)
-        v_pool = [sb.tile([P, TOKENS], F32, name="v_pool%d" % h, align_bytes=64) for h in range(halves)]
         q_codes = sb.tile([P, NQ], U32, name="q_codes", align_bytes=64)
         q_plane = sb.tile([P, NQ], U8, name="q_plane", align_bytes=64)
         og_sb = sb.tile([P, DV], F32, name="og_sb", align_bytes=64)
         ident = sb.tile([P, P], F32, name="ident", align_bytes=64)
 
         nc.vector.memset(ks_pool[:].bitcast(I32), 0)
-        nc.vector.memset(vs_pool[:], 0.0)
-        nc.gpsimd.memset(q_plane[:].bitcast(I32), 0)
+        nc.vector.memset(q_plane[:].bitcast(I32), 0)
+        nc.vector.memset(vs_pool[:].bitcast(I32), 0)
         make_identity(nc, ident[:])
 
+        def load_scale_rows(queue, plane, rows, quad):
+            queue.dma_start(plane[:].bitcast(I32)[32 * quad : 32 * quad + 4, :], rows[4 * quad : 4 * quad + 4, :].bitcast(I32))
+
         nc.sync.dma_start(offsets[:], offs)
+        nc.scalar.dma_start(og_sb[:], og[0])
         nc.sync.dma_start(q_codes[:].bitcast(I32), q_words[0, 0].rearrange("g q r -> g (q r)").bitcast(I32))
         for quad in range(4):
-            nc.scalar.dma_start(ks_pool[:].bitcast(I32)[32 * quad : 32 * quad + 4, :], k_scales[0, 4 * quad : 4 * quad + 4, :].bitcast(I32))
+            load_scale_rows(nc.sync if quad < 2 else nc.scalar, ks_pool, k_scales[0], quad)
         nc.sync.dma_start(k_pool[:].bitcast(I32), k_words[0].rearrange("g t r -> g (t r)").bitcast(I32))
-        nc.sync.dma_start(v_pool[0][:], vT[0:P, :])
-        nc.scalar.dma_start(vs_pool[VS_ROW : VS_ROW + 1, :], vs[0:1, :])
-        nc.sync.dma_start(v_pool[1][:], vT[P : 2 * P, :])
         for quad in range(4):
-            nc.scalar.dma_start(q_plane[:].bitcast(I32)[32 * quad : 32 * quad + 4, :], q_scales[0, 0, 4 * quad : 4 * quad + 4, :].bitcast(I32))
-        nc.sync.dma_start(og_sb[:], og[0])
+            load_scale_rows(nc.sync, q_plane, q_scales[0, 0], quad)
+        nc.sync.dma_start(vs_pool[VS_ROW : VS_ROW + 1, :], vs[0:1, :])
+
+        gate = sb.tile([P, DV], F32, name="gate", align_bytes=64)
+        nc.scalar.activation(gate[:], og_sb[:], ACT.Sigmoid)
+        v_pool = [reuse.tile([P, TOKENS], F32, name="v_pool%d" % h, offset=4 * TOKENS * h, align_bytes=64) for h in range(halves)]
+        for h in range(halves):
+            nc.sync.dma_start(v_pool[h][:], vT[h * P : (h + 1) * P, :])
 
         ks_g = sb.tile([P, SLOTS], U8, name="ks_g", align_bytes=64)
         nc.vector.tensor_copy(ks_g[:], ks_pool[:].indirect(offsets[:]))
         k_plane = sb.tile([P, PACK, P], U8, name="k_plane", align_bytes=64)
         nc.vector.tensor_copy(k_plane[:].rearrange("p t s -> p s t"), ks_g[:].rearrange("p (s t) -> p s t", t=PACK))
-        vs_g = sb.tile([P, SLOTS], F32, name="vs_g", align_bytes=64)
-        nc.vector.tensor_copy(vs_g[:], vs_pool[:].indirect(offsets[:]))
         k_codes = sb.tile([P, PACK, P], U32, name="k_codes", align_bytes=64)
         nc.vector.tensor_copy(k_codes[:].rearrange("p t s -> p s t"), k_pool[:].indirect(offsets[:]))
 
-        vs_bank = ps.tile([P, PACK, P], F32, name="vs_bank")
-        for t in range(PACK):
-            nc.tensor.transpose(vs_bank[:, t, :], vs_g[:, t:SLOTS:PACK], ident[:])
+        vs_g = sb.tile([P, SLOTS], F32, name="vs_g", align_bytes=64)
+        nc.vector.tensor_copy(vs_g[:], vs_pool[:].indirect(offsets[:]))
+        v_g = [sb.tile([P, SLOTS], BF16, name="v_g%d" % h, align_bytes=64) for h in range(halves)]
+        for h in range(halves):
+            nc.vector.tensor_copy(v_g[h][:], v_pool[h][:].indirect(offsets[:]))
 
         scores = ps.tile([P, PACK, NQ], F32, name="scores")
         for t in range(PACK):
             nc.tensor.matmul_mx(out=scores[:, t, :], lhsT=k_codes[:, t, :].bitcast(FP8X4), lhsT_scale=k_plane[:, t, :],
                                 rhs=q_codes[:].bitcast(FP8X4), rhs_scale=q_plane[:], start=True, stop=True)
+        vs_bank = ps.tile([P, PACK, P], F32, name="vs_bank")
+        for t in range(PACK):
+            nc.tensor.transpose(vs_bank[:, t, :], vs_g[:, t:SLOTS:PACK], ident[:])
         p_sb = sb.tile([P, NQ, PACK], F32, name="p_sb", align_bytes=64)
         nc.scalar.activation(p_sb[:], scores[:].rearrange("p t q -> p q t"), ACT.Silu)
-        w_bf = sb.tile([P, NQ, PACK], BF16, name="w_bf", align_bytes=64)
+        w_bf = reuse.tile([P, NQ, PACK], BF16, name="w_bf", offset=4 * TOKENS, align_bytes=64)
         vs_cols = vs_bank[:, :, VS_ROW : VS_ROW + 1].rearrange("p t o -> p o t").to_broadcast([P, NQ, PACK])
         nc.vector.tensor_tensor(w_bf[:], p_sb[:], vs_cols, MULT)
         w_codes = sb.tile([P, NQ], U32, name="w_codes", align_bytes=64)
         w_plane = sb.tile([P, NQ], U8, name="w_plane", align_bytes=64)
-        nc.vector.quantize_mx(out=w_codes[:].bitcast(FP8X4), scales=w_plane[:], in_=w_bf[:].rearrange("p q t -> p (q t)"))
 
-        gate = sb.tile([P, DV], F32, name="gate", align_bytes=64)
-        nc.scalar.activation(gate[:], og_sb[:], ACT.Sigmoid)
-
+        v_bf = []
         for h in range(halves):
-            cols = slice(h * P, (h + 1) * P)
-            v_g = sb.tile([P, SLOTS], BF16, name="v_g%d" % h, align_bytes=64)
-            nc.vector.tensor_copy(v_g[:], v_pool[h][:].indirect(offsets[:]))
-            pairs = v_g[:].bitcast(F32)
+            pairs = v_g[h][:].bitcast(F32)
             v_bank = ps.tile([P, 2, P], F32, name="v_bank%d" % h)
             for u in range(2):
                 nc.tensor.transpose(v_bank[:, u, :], pairs[:, u : SLOTS // 2 : 2], ident[:])
-            v_bf = sb.tile([P, P * PACK], BF16, name="v_bf%d" % h, align_bytes=64)
-            nc.scalar.copy(v_bf[:].bitcast(F32).rearrange("p (e u) -> p e u", u=2), v_bank[:].rearrange("p u e -> p e u"))
-            v_codes = sb.tile([P, P], U32, name="v_codes%d" % h, align_bytes=64)
-            v_plane = sb.tile([P, P], U8, name="v_plane%d" % h, align_bytes=64)
-            nc.vector.quantize_mx(out=v_codes[:].bitcast(FP8X4), scales=v_plane[:], in_=v_bf[:])
+            v_bf.append(sb.tile([P, P * PACK], BF16, name="v_bf%d" % h, align_bytes=64))
+            nc.scalar.copy(v_bf[h][:].bitcast(F32).rearrange("p (e u) -> p e u", u=2), v_bank[:].rearrange("p u e -> p e u"))
+
+        v_codes = [reuse.tile([P, P], U32, name="v_codes%d" % h, offset=4 * TOKENS + 1024 + 512 * h, align_bytes=64) for h in range(halves)]
+        v_plane = [sb.tile([P, P], U8, name="v_plane%d" % h, align_bytes=64) for h in range(halves)]
+        nc.vector.quantize_mx(out=v_codes[0][:].bitcast(FP8X4), scales=v_plane[0][:], in_=v_bf[0][:])
+        nc.vector.quantize_mx(out=w_codes[:].bitcast(FP8X4), scales=w_plane[:], in_=w_bf[:].rearrange("p q t -> p (q t)"))
+        nc.vector.quantize_mx(out=v_codes[1][:].bitcast(FP8X4), scales=v_plane[1][:], in_=v_bf[1][:])
+
+        for h in range(halves):
+            cols = slice(h * P, (h + 1) * P)
             y_bank = ps.tile([P, P], F32, name="y_bank%d" % h)
             nc.tensor.matmul_mx(out=y_bank[:], lhsT=w_codes[:].bitcast(FP8X4), lhsT_scale=w_plane[:],
-                                rhs=v_codes[:].bitcast(FP8X4), rhs_scale=v_plane[:], start=True, stop=True)
+                                rhs=v_codes[h][:].bitcast(FP8X4), rhs_scale=v_plane[h][:], start=True, stop=True)
             res = sb.tile([P, P], F32, name="res%d" % h, align_bytes=64)
             nc.vector.scalar_tensor_tensor(res[:], y_bank[:], 1.0 / 16.0, gate[:, cols], MULT, MULT)
             nc.sync.dma_start(out[0, :, cols], res[:])

@@ -42,62 +42,69 @@ def tile_attend_silu_gate_srtq128n512t2048_kernel(tc, q_words, q_scales, k_words
         nc.vector.memset(ks_pool[:].bitcast(I32), 0)
         nc.vector.memset(q_plane[:].bitcast(I32), 0)
         nc.vector.memset(vs_pool[:].bitcast(I32), 0)
-        make_identity(nc, ident[:])
+        nc.vector.memset(ident[:], 0.0)
+        make_identity(nc, ident[:], nomemset=True)
 
         def load_scale_rows(queue, plane, rows, quad):
             queue.dma_start(plane[:].bitcast(I32)[32 * quad : 32 * quad + 4, :], rows[4 * quad : 4 * quad + 4, :].bitcast(I32))
 
+        v_pool = [reuse.tile([P, TOKENS], F32, name="v_pool%d" % h, offset=4 * TOKENS * h, align_bytes=64) for h in range(halves)]
         nc.sync.dma_start(offsets[:], offs)
-        nc.scalar.dma_start(og_sb[:], og[0])
-        nc.sync.dma_start(q_codes[:].bitcast(I32), q_words[0, 0].rearrange("g q r -> g (q r)").bitcast(I32))
-        for quad in range(4):
-            load_scale_rows(nc.sync if quad < 2 else nc.scalar, ks_pool, k_scales[0], quad)
+        nc.scalar.dma_start(q_codes[:].bitcast(I32), q_words[0, 0].rearrange("g q r -> g (q r)").bitcast(I32))
         nc.sync.dma_start(k_pool[:].bitcast(I32), k_words[0].rearrange("g t r -> g (t r)").bitcast(I32))
         for quad in range(4):
+            load_scale_rows(nc.scalar, ks_pool, k_scales[0], quad)
+        nc.scalar.dma_start(vs_pool[VS_ROW : VS_ROW + 1, :], vs[0:1, :])
+        load_scale_rows(nc.sync, q_plane, q_scales[0, 0], 0)
+        nc.sync.dma_start(v_pool[0][:], vT[0:P, :])
+        for quad in range(1, 4):
             load_scale_rows(nc.sync, q_plane, q_scales[0, 0], quad)
-        nc.sync.dma_start(vs_pool[VS_ROW : VS_ROW + 1, :], vs[0:1, :])
+        nc.sync.dma_start(v_pool[1][:], vT[P : 2 * P, :])
+        nc.sync.dma_start(og_sb[:], og[0])
 
-        gate = sb.tile([P, DV], F32, name="gate", align_bytes=64)
-        nc.scalar.activation(gate[:], og_sb[:], ACT.Sigmoid)
-        v_pool = [reuse.tile([P, TOKENS], F32, name="v_pool%d" % h, offset=4 * TOKENS * h, align_bytes=64) for h in range(halves)]
-        for h in range(halves):
-            nc.sync.dma_start(v_pool[h][:], vT[h * P : (h + 1) * P, :])
-
-        ks_g = sb.tile([P, SLOTS], U8, name="ks_g", align_bytes=64)
-        nc.vector.tensor_copy(ks_g[:], ks_pool[:].indirect(offsets[:]))
-        k_plane = sb.tile([P, PACK, P], U8, name="k_plane", align_bytes=64)
-        nc.vector.tensor_copy(k_plane[:].rearrange("p t s -> p s t"), ks_g[:].rearrange("p (s t) -> p s t", t=PACK))
-        k_codes = sb.tile([P, PACK, P], U32, name="k_codes", align_bytes=64)
-        nc.vector.tensor_copy(k_codes[:].rearrange("p t s -> p s t"), k_pool[:].indirect(offsets[:]))
-
+        k_plane = sb.tile([P, SLOTS], U8, name="k_plane", align_bytes=64)
+        nc.vector.tensor_copy(k_plane[:], ks_pool[:].indirect(offsets[:]))
+        k_codes = sb.tile([P, SLOTS], U32, name="k_codes", align_bytes=64)
+        nc.vector.tensor_copy(k_codes[:], k_pool[:].indirect(offsets[:]))
         vs_g = sb.tile([P, SLOTS], F32, name="vs_g", align_bytes=64)
         nc.vector.tensor_copy(vs_g[:], vs_pool[:].indirect(offsets[:]))
         v_g = [sb.tile([P, SLOTS], BF16, name="v_g%d" % h, align_bytes=64) for h in range(halves)]
         for h in range(halves):
             nc.vector.tensor_copy(v_g[h][:], v_pool[h][:].indirect(offsets[:]))
 
-        scores = ps.tile([P, PACK, NQ], F32, name="scores")
-        for t in range(PACK):
-            nc.tensor.matmul_mx(out=scores[:, t, :], lhsT=k_codes[:, t, :].bitcast(FP8X4), lhsT_scale=k_plane[:, t, :],
-                                rhs=q_codes[:].bitcast(FP8X4), rhs_scale=q_plane[:], start=True, stop=True)
-        vs_bank = ps.tile([P, PACK, P], F32, name="vs_bank")
+        scores = ps.tile([NQ, SLOTS], F32, name="scores", tag="scores_bank")
+        nc.tensor.matmul_mx(out=scores[:], lhsT=q_codes[:].bitcast(FP8X4), lhsT_scale=q_plane[:],
+                            rhs=k_codes[:].bitcast(FP8X4), rhs_scale=k_plane[:], start=True, stop=True)
+        p_sb = sb.tile([NQ, PACK, P], F32, name="p_sb", align_bytes=64)
+        nc.scalar.activation(p_sb[:], scores[:].rearrange("q (s t) -> q t s", t=PACK), ACT.Silu)
+
+        vs_bank = ps.tile([P, PACK, P], F32, name="vs_bank", tag="scores_bank")
         for t in range(PACK):
             nc.tensor.transpose(vs_bank[:, t, :], vs_g[:, t:SLOTS:PACK], ident[:])
-        p_sb = sb.tile([P, NQ, PACK], F32, name="p_sb", align_bytes=64)
-        nc.scalar.activation(p_sb[:], scores[:].rearrange("p t q -> p q t"), ACT.Silu)
+        vs_cols = sb.tile([P, 1, PACK], F32, name="vs_cols", align_bytes=64)
+        nc.scalar.copy(vs_cols[:], vs_bank[:, :, VS_ROW : VS_ROW + 1].rearrange("p t o -> p o t"))
+
+        p_bank = ps.tile([P, PACK, NQ], F32, name="p_bank")
+        for t in range(PACK):
+            nc.tensor.transpose(p_bank[:, t, :], p_sb[:, t, :], ident[:])
         w_bf = reuse.tile([P, NQ, PACK], BF16, name="w_bf", offset=4 * TOKENS, align_bytes=64)
-        vs_cols = vs_bank[:, :, VS_ROW : VS_ROW + 1].rearrange("p t o -> p o t").to_broadcast([P, NQ, PACK])
-        nc.vector.tensor_tensor(w_bf[:], p_sb[:], vs_cols, MULT)
+        nc.vector.tensor_tensor(w_bf[:], p_bank[:].rearrange("p t q -> p q t"), vs_cols[:].to_broadcast([P, NQ, PACK]), MULT)
+
+        half_tanh = reuse.tile([P, DV], F32, name="half_tanh", offset=8 * TOKENS + 512, align_bytes=64)
+        gate = sb.tile([P, DV], F32, name="gate", align_bytes=64)
+        nc.scalar.activation(half_tanh[:], og_sb[:], ACT.Tanh, scale=0.5)
+        nc.scalar.activation(gate[:], half_tanh[:], ACT.Copy, scale=1.0 / 32.0, bias=1.0 / 32.0)
+
         w_codes = sb.tile([P, NQ], U32, name="w_codes", align_bytes=64)
         w_plane = sb.tile([P, NQ], U8, name="w_plane", align_bytes=64)
 
         v_bf = []
         for h in range(halves):
             pairs = v_g[h][:].bitcast(F32)
-            v_bank = ps.tile([P, 2, P], F32, name="v_bank%d" % h)
+            v_bank = ps.tile([P, 2, P], F32, name="v_bank%d" % h, tag="scores_bank" if h == 0 else "v_bank1")
             for u in range(2):
                 nc.tensor.transpose(v_bank[:, u, :], pairs[:, u : SLOTS // 2 : 2], ident[:])
-            v_bf.append(sb.tile([P, P * PACK], BF16, name="v_bf%d" % h, align_bytes=64))
+            v_bf.append(reuse.tile([P, P * PACK], BF16, name="v_bf%d" % h, offset=8 * TOKENS + 1024 * h, align_bytes=64))
             nc.scalar.copy(v_bf[h][:].bitcast(F32).rearrange("p (e u) -> p e u", u=2), v_bank[:].rearrange("p u e -> p e u"))
 
         v_codes = [reuse.tile([P, P], U32, name="v_codes%d" % h, offset=4 * TOKENS + 1024 + 512 * h, align_bytes=64) for h in range(halves)]
@@ -112,5 +119,5 @@ def tile_attend_silu_gate_srtq128n512t2048_kernel(tc, q_words, q_scales, k_words
             nc.tensor.matmul_mx(out=y_bank[:], lhsT=w_codes[:].bitcast(FP8X4), lhsT_scale=w_plane[:],
                                 rhs=v_codes[h][:].bitcast(FP8X4), rhs_scale=v_plane[h][:], start=True, stop=True)
             res = sb.tile([P, P], F32, name="res%d" % h, align_bytes=64)
-            nc.vector.scalar_tensor_tensor(res[:], y_bank[:], 1.0 / 16.0, gate[:, cols], MULT, MULT)
+            nc.vector.tensor_tensor(res[:], y_bank[:], gate[:, cols], MULT)
             nc.sync.dma_start(out[0, :, cols], res[:])

@@ -17,6 +17,7 @@ P = 128
 PACK = 4
 SLOTS, TOKENS, D, DV, NQ = 512, 2048, 512, 256, 128
 VS_ROW = 8
+FIRST_TOKENS = 512
 
 FLOPS = 2 * NQ * SLOTS * D + 2 * NQ * SLOTS * DV
 BYTES = D * TOKENS + D // 32 * TOKENS + D * NQ + D // 32 * NQ + 4 * DV * TOKENS + 4 * TOKENS + 2 * 4 * NQ * DV + 2 * P * SLOTS // 16
@@ -49,15 +50,16 @@ def tile_attend_silu_gate_srtq128n512t2048_kernel(tc, q_words, q_scales, k_words
             queue.dma_start(plane[:].bitcast(I32)[32 * quad : 32 * quad + 4, :], rows[4 * quad : 4 * quad + 4, :].bitcast(I32))
 
         v_pool = [reuse.tile([P, TOKENS], F32, name="v_pool%d" % h, offset=4 * TOKENS * h, align_bytes=64) for h in range(halves)]
+        k_rows = k_words[0].rearrange("g t r -> g (t r)").bitcast(I32)
         nc.sync.dma_start(offsets[:], offs)
-        nc.scalar.dma_start(q_codes[:].bitcast(I32), q_words[0, 0].rearrange("g q r -> g (q r)").bitcast(I32))
-        nc.sync.dma_start(k_pool[:].bitcast(I32), k_words[0].rearrange("g t r -> g (t r)").bitcast(I32))
+        nc.sync.dma_start(k_pool[:].bitcast(I32)[:, :FIRST_TOKENS], k_rows[:, :FIRST_TOKENS])
         for quad in range(4):
-            load_scale_rows(nc.scalar, ks_pool, k_scales[0], quad)
-        nc.scalar.dma_start(vs_pool[VS_ROW : VS_ROW + 1, :], vs[0:1, :])
-        load_scale_rows(nc.sync, q_plane, q_scales[0, 0], 0)
+            load_scale_rows(nc.sync if quad < 2 else nc.scalar, ks_pool, k_scales[0], quad)
+        nc.sync.dma_start(k_pool[:].bitcast(I32)[:, FIRST_TOKENS:], k_rows[:, FIRST_TOKENS:])
+        nc.sync.dma_start(vs_pool[VS_ROW : VS_ROW + 1, :], vs[0:1, :])
         nc.sync.dma_start(v_pool[0][:], vT[0:P, :])
-        for quad in range(1, 4):
+        nc.sync.dma_start(q_codes[:].bitcast(I32), q_words[0, 0].rearrange("g q r -> g (q r)").bitcast(I32))
+        for quad in range(4):
             load_scale_rows(nc.sync, q_plane, q_scales[0, 0], quad)
         nc.sync.dma_start(v_pool[1][:], vT[P : 2 * P, :])
         nc.sync.dma_start(og_sb[:], og[0])

@@ -17,6 +17,8 @@ P = 128
 PACK = 4
 SLOTS, TOKENS, D, DV, NQ = 512, 2048, 512, 256, 128
 VS_ROW = 8
+EARLY_SLOTS = SLOTS // 2
+EARLY_TOKENS = TOKENS - SLOTS + EARLY_SLOTS
 FIRST_TOKENS = 512
 
 FLOPS = 2 * NQ * SLOTS * D + 2 * NQ * SLOTS * DV
@@ -34,7 +36,7 @@ def tile_attend_silu_gate_srtq128n512t2048_kernel(tc, q_words, q_scales, k_words
         offsets = sb.tile([P, SLOTS // 16], U16, name="offsets")
         k_pool = sb.tile([P, TOKENS], U32, name="k_pool", align_bytes=64)
         ks_pool = sb.tile([P, TOKENS], U8, name="ks_pool", align_bytes=64)
-        vs_pool = sb.tile([P, TOKENS], F32, name="vs_pool", align_bytes=64)
+        vs_pool = sb.tile([P, TOKENS], F32, name="vs_pool", tag="vs_then_keys", align_bytes=64)
         q_codes = sb.tile([P, NQ], U32, name="q_codes", align_bytes=64)
         q_plane = sb.tile([P, NQ], U8, name="q_plane", align_bytes=64)
         og_sb = sb.tile([P, DV], F32, name="og_sb", align_bytes=64)
@@ -61,18 +63,21 @@ def tile_attend_silu_gate_srtq128n512t2048_kernel(tc, q_words, q_scales, k_words
         nc.sync.dma_start(q_codes[:].bitcast(I32), q_words[0, 0].rearrange("g q r -> g (q r)").bitcast(I32))
         for quad in range(4):
             load_scale_rows(nc.sync, q_plane, q_scales[0, 0], quad)
-        nc.sync.dma_start(v_pool[1][:], vT[P : 2 * P, :])
+        nc.sync.dma_start(v_pool[1][:, :EARLY_TOKENS], vT[P : 2 * P, :EARLY_TOKENS])
+        nc.sync.dma_start(v_pool[1][:, EARLY_TOKENS:], vT[P : 2 * P, EARLY_TOKENS:])
         nc.sync.dma_start(og_sb[:], og[0])
 
         k_plane = sb.tile([P, SLOTS], U8, name="k_plane", align_bytes=64)
         nc.vector.tensor_copy(k_plane[:], ks_pool[:].indirect(offsets[:]))
-        k_codes = sb.tile([P, SLOTS], U32, name="k_codes", align_bytes=64)
-        nc.vector.tensor_copy(k_codes[:], k_pool[:].indirect(offsets[:]))
         vs_g = sb.tile([P, SLOTS], F32, name="vs_g", align_bytes=64)
         nc.vector.tensor_copy(vs_g[:], vs_pool[:].indirect(offsets[:]))
+        k_codes = sb.tile([P, SLOTS], U32, name="k_codes", tag="vs_then_keys", align_bytes=64)
+        nc.vector.tensor_copy(k_codes[:], k_pool[:].indirect(offsets[:]))
         v_g = [sb.tile([P, SLOTS], BF16, name="v_g%d" % h, align_bytes=64) for h in range(halves)]
-        for h in range(halves):
-            nc.vector.tensor_copy(v_g[h][:], v_pool[h][:].indirect(offsets[:]))
+        nc.vector.tensor_copy(v_g[0][:], v_pool[0][:].indirect(offsets[:]))
+        v_early = sb.tile([P, EARLY_SLOTS], F32, name="v_early", align_bytes=64)
+        nc.vector.tensor_copy(v_early[:], v_pool[1][:, :EARLY_TOKENS].indirect(offsets[:, : EARLY_SLOTS // 16]))
+        nc.vector.tensor_copy(v_g[1][:, EARLY_SLOTS:], v_pool[1][:].indirect(offsets[:, EARLY_SLOTS // 16 :]))
 
         scores = ps.tile([NQ, SLOTS], F32, name="scores", tag="scores_bank")
         nc.tensor.matmul_mx(out=scores[:], lhsT=q_codes[:].bitcast(FP8X4), lhsT_scale=q_plane[:],
@@ -80,11 +85,13 @@ def tile_attend_silu_gate_srtq128n512t2048_kernel(tc, q_words, q_scales, k_words
         p_sb = sb.tile([NQ, PACK, P], F32, name="p_sb", align_bytes=64)
         nc.scalar.activation(p_sb[:], scores[:].rearrange("q (s t) -> q t s", t=PACK), ACT.Silu)
 
-        vs_bank = ps.tile([P, PACK, P], F32, name="vs_bank", tag="scores_bank")
+        nc.scalar.copy(v_g[1][:, :EARLY_SLOTS], v_early[:])
+
+        vs_bank = ps.tile([P, PACK, P], F32, name="vs_bank")
         for t in range(PACK):
             nc.tensor.transpose(vs_bank[:, t, :], vs_g[:, t:SLOTS:PACK], ident[:])
         vs_cols = sb.tile([P, 1, PACK], F32, name="vs_cols", align_bytes=64)
-        nc.scalar.copy(vs_cols[:], vs_bank[:, :, VS_ROW : VS_ROW + 1].rearrange("p t o -> p o t"))
+        nc.vector.tensor_copy(vs_cols[:], vs_bank[:, :, VS_ROW : VS_ROW + 1].rearrange("p t o -> p o t"))
 
         p_bank = ps.tile([P, PACK, NQ], F32, name="p_bank")
         for t in range(PACK):

from contextlib import ExitStack

import concourse.mybir as mybir
from concourse.masks import make_identity

F32 = mybir.dt.float32
BF16 = mybir.dt.bfloat16
I32 = mybir.dt.int32
U32 = mybir.dt.uint32
U16 = mybir.dt.uint16
U8 = mybir.dt.uint8
FP8X4 = mybir.dt.float8_e4m3fn_x4
ACT = mybir.ActivationFunctionType
MULT = mybir.AluOpType.mult

P = 128
PACK = 4
SLOTS, TOKENS, D, DV, NQ = 512, 2048, 512, 256, 128
VS_ROW = 8
EARLY_SLOTS = SLOTS // 2
EARLY_TOKENS = TOKENS - SLOTS + EARLY_SLOTS
FIRST_TOKENS = 512

FLOPS = 2 * NQ * SLOTS * D + 2 * NQ * SLOTS * DV
BYTES = D * TOKENS + D // 32 * TOKENS + D * NQ + D // 32 * NQ + 4 * DV * TOKENS + 4 * TOKENS + 2 * 4 * NQ * DV + 2 * P * SLOTS // 16


def tile_attend_silu_gate_srtq128n512t2048_kernel(tc, q_words, q_scales, k_words, k_scales, vT, vs, og, offs, out):
    nc = tc.nc
    halves = DV // P
    with ExitStack() as ctx:
        sb = ctx.enter_context(tc.tile_pool(name="sb", bufs=1))
        reuse = ctx.enter_context(tc.tile_pool(name="reuse", bufs=1))
        ps = ctx.enter_context(tc.psum_pool(name="ps", bufs=1))

        offsets = sb.tile([P, SLOTS // 16], U16, name="offsets")
        k_pool = sb.tile([P, TOKENS], U32, name="k_pool", align_bytes=64)
        ks_pool = sb.tile([P, TOKENS], U8, name="ks_pool", align_bytes=64)
        vs_pool = sb.tile([P, TOKENS], F32, name="vs_pool", tag="vs_then_keys", align_bytes=64)
        q_codes = sb.tile([P, NQ], U32, name="q_codes", align_bytes=64)
        q_plane = sb.tile([P, NQ], U8, name="q_plane", align_bytes=64)
        og_sb = sb.tile([P, DV], F32, name="og_sb", align_bytes=64)
        ident = sb.tile([P, P], F32, name="ident", align_bytes=64)

        nc.vector.memset(ks_pool[:].bitcast(I32), 0)
        nc.vector.memset(q_plane[:].bitcast(I32), 0)
        nc.vector.memset(vs_pool[:].bitcast(I32), 0)
        nc.vector.memset(ident[:], 0.0)
        make_identity(nc, ident[:], nomemset=True)

        def load_scale_rows(queue, plane, rows, quad):
            queue.dma_start(plane[:].bitcast(I32)[32 * quad : 32 * quad + 4, :], rows[4 * quad : 4 * quad + 4, :].bitcast(I32))

        v_pool = [reuse.tile([P, TOKENS], F32, name="v_pool%d" % h, offset=4 * TOKENS * h, align_bytes=64) for h in range(halves)]
        k_rows = k_words[0].rearrange("g t r -> g (t r)").bitcast(I32)
        nc.sync.dma_start(offsets[:], offs)
        nc.sync.dma_start(k_pool[:].bitcast(I32)[:, :FIRST_TOKENS], k_rows[:, :FIRST_TOKENS])
        for quad in range(4):
            load_scale_rows(nc.sync if quad < 2 else nc.scalar, ks_pool, k_scales[0], quad)
        nc.sync.dma_start(k_pool[:].bitcast(I32)[:, FIRST_TOKENS:], k_rows[:, FIRST_TOKENS:])
        nc.sync.dma_start(vs_pool[VS_ROW : VS_ROW + 1, :], vs[0:1, :])
        nc.sync.dma_start(v_pool[0][:], vT[0:P, :])
        nc.sync.dma_start(q_codes[:].bitcast(I32), q_words[0, 0].rearrange("g q r -> g (q r)").bitcast(I32))
        for quad in range(4):
            load_scale_rows(nc.sync, q_plane, q_scales[0, 0], quad)
        nc.sync.dma_start(v_pool[1][:, :EARLY_TOKENS], vT[P : 2 * P, :EARLY_TOKENS])
        nc.sync.dma_start(v_pool[1][:, EARLY_TOKENS:], vT[P : 2 * P, EARLY_TOKENS:])
        nc.sync.dma_start(og_sb[:], og[0])

        k_plane = sb.tile([P, SLOTS], U8, name="k_plane", align_bytes=64)
        nc.vector.tensor_copy(k_plane[:], ks_pool[:].indirect(offsets[:]))
        vs_g = sb.tile([P, SLOTS], F32, name="vs_g", align_bytes=64)
        nc.vector.tensor_copy(vs_g[:], vs_pool[:].indirect(offsets[:]))
        k_codes = sb.tile([P, SLOTS], U32, name="k_codes", tag="vs_then_keys", align_bytes=64)
        nc.vector.tensor_copy(k_codes[:], k_pool[:].indirect(offsets[:]))
        v_g = [sb.tile([P, SLOTS], BF16, name="v_g%d" % h, align_bytes=64) for h in range(halves)]
        nc.vector.tensor_copy(v_g[0][:], v_pool[0][:].indirect(offsets[:]))
        v_early = sb.tile([P, EARLY_SLOTS], F32, name="v_early", align_bytes=64)
        nc.vector.tensor_copy(v_early[:], v_pool[1][:, :EARLY_TOKENS].indirect(offsets[:, : EARLY_SLOTS // 16]))
        nc.vector.tensor_copy(v_g[1][:, EARLY_SLOTS:], v_pool[1][:].indirect(offsets[:, EARLY_SLOTS // 16 :]))

        scores = ps.tile([NQ, SLOTS], F32, name="scores", tag="scores_bank")
        nc.tensor.matmul_mx(out=scores[:], lhsT=q_codes[:].bitcast(FP8X4), lhsT_scale=q_plane[:],
                            rhs=k_codes[:].bitcast(FP8X4), rhs_scale=k_plane[:], start=True, stop=True)
        p_sb = sb.tile([NQ, PACK, P], F32, name="p_sb", align_bytes=64)
        nc.scalar.activation(p_sb[:], scores[:].rearrange("q (s t) -> q t s", t=PACK), ACT.Silu)

        nc.scalar.copy(v_g[1][:, :EARLY_SLOTS], v_early[:])

        vs_bank = ps.tile([P, PACK, P], F32, name="vs_bank")
        for t in range(PACK):
            nc.tensor.transpose(vs_bank[:, t, :], vs_g[:, t:SLOTS:PACK], ident[:])
        vs_cols = sb.tile([P, 1, PACK], F32, name="vs_cols", align_bytes=64)
        nc.vector.tensor_copy(vs_cols[:], vs_bank[:, :, VS_ROW : VS_ROW + 1].rearrange("p t o -> p o t"))

        p_bank = ps.tile([P, PACK, NQ], F32, name="p_bank")
        for t in range(PACK):
            nc.tensor.transpose(p_bank[:, t, :], p_sb[:, t, :], ident[:])
        w_bf = reuse.tile([P, NQ, PACK], BF16, name="w_bf", offset=4 * TOKENS, align_bytes=64)
        nc.vector.tensor_tensor(w_bf[:], p_bank[:].rearrange("p t q -> p q t"), vs_cols[:].to_broadcast([P, NQ, PACK]), MULT)

        half_tanh = reuse.tile([P, DV], F32, name="half_tanh", offset=8 * TOKENS + 512, align_bytes=64)
        gate = sb.tile([P, DV], F32, name="gate", align_bytes=64)
        nc.scalar.activation(half_tanh[:], og_sb[:], ACT.Tanh, scale=0.5)
        nc.scalar.activation(gate[:], half_tanh[:], ACT.Copy, scale=1.0 / 32.0, bias=1.0 / 32.0)

        w_codes = sb.tile([P, NQ], U32, name="w_codes", align_bytes=64)
        w_plane = sb.tile([P, NQ], U8, name="w_plane", align_bytes=64)

        v_bf = []
        for h in range(halves):
            pairs = v_g[h][:].bitcast(F32)
            v_bank = ps.tile([P, 2, P], F32, name="v_bank%d" % h, tag="scores_bank" if h == 0 else "v_bank1")
            for u in range(2):
                nc.tensor.transpose(v_bank[:, u, :], pairs[:, u : SLOTS // 2 : 2], ident[:])
            v_bf.append(reuse.tile([P, P * PACK], BF16, name="v_bf%d" % h, offset=8 * TOKENS + 1024 * h, align_bytes=64))
            nc.scalar.copy(v_bf[h][:].bitcast(F32).rearrange("p (e u) -> p e u", u=2), v_bank[:].rearrange("p u e -> p e u"))

        v_codes = [reuse.tile([P, P], U32, name="v_codes%d" % h, offset=4 * TOKENS + 1024 + 512 * h, align_bytes=64) for h in range(halves)]
        v_plane = [sb.tile([P, P], U8, name="v_plane%d" % h, align_bytes=64) for h in range(halves)]
        nc.vector.quantize_mx(out=v_codes[0][:].bitcast(FP8X4), scales=v_plane[0][:], in_=v_bf[0][:])
        nc.vector.quantize_mx(out=w_codes[:].bitcast(FP8X4), scales=w_plane[:], in_=w_bf[:].rearrange("p q t -> p (q t)"))
        nc.vector.quantize_mx(out=v_codes[1][:].bitcast(FP8X4), scales=v_plane[1][:], in_=v_bf[1][:])

        for h in range(halves):
            cols = slice(h * P, (h + 1) * P)
            y_bank = ps.tile([P, P], F32, name="y_bank%d" % h)
            nc.tensor.matmul_mx(out=y_bank[:], lhsT=w_codes[:].bitcast(FP8X4), lhsT_scale=w_plane[:],
                                rhs=v_codes[h][:].bitcast(FP8X4), rhs_scale=v_plane[h][:], start=True, stop=True)
            res = sb.tile([P, P], F32, name="res%d" % h, align_bytes=64)
            nc.vector.tensor_tensor(res[:], y_bank[:], gate[:, cols], MULT)
            nc.sync.dma_start(out[0, :, cols], res[:])
